import numpy as np
import ml_dtypes


def mxq(x, axis, fmt="e4m3"):
    dtype, down = {"e4m3": (ml_dtypes.float8_e4m3fn, 7), "e5m2": (ml_dtypes.float8_e5m2, 14)}[fmt]
    v = np.moveaxis(np.asarray(x, np.float32).astype(ml_dtypes.bfloat16).astype(np.float64), axis, -1)
    blocks = v.reshape(v.shape[:-1] + (-1, 32))
    amax = np.abs(blocks).max(-1, keepdims=True)
    byte = np.maximum(np.where(amax > 0, np.frexp(amax)[1] - 1 + 127, 0) - down, 1)
    scale = np.exp2(byte - 127.0)
    codes = (blocks / scale).astype(np.float32).astype(dtype).astype(np.float64)
    return np.moveaxis((codes * scale).reshape(v.shape), -1, axis)


WIDE = False


def mx_kscale(k):
    if not WIDE:
        return np.ones(k)
    levels = np.array([10, -10, 5, -5, 0])
    if k % 512:
        return np.exp2(np.random.permutation(np.resize(levels, k // 32))).repeat(32)
    a = np.empty((k // 512, 16))
    for p in range(k // 512):
        a[p, :8] = np.random.permutation(np.resize(levels, 8))
        for g in range(8):
            far = levels[np.abs(levels - a[p, g]) >= 10]
            a[p, g + 8] = far[np.random.randint(len(far))]
    return np.exp2(a.ravel()).repeat(32)


def f64(x):
    return np.asarray(x).astype(np.float64)


def striped(idx):
    return np.tile(idx.reshape(-1, 16).T, (8, 1)).astype(np.uint16)


def unstriped(offs):
    return offs[:16].T.reshape(-1).astype(np.int64)


E2M1 = np.array([0.0, 0.5, 1.0, 1.5, 2.0, 3.0, 4.0, 6.0, -0.0, -0.5, -1.0, -1.5, -2.0, -3.0, -4.0, -6.0])


def pack_weight(w, fmt):
    k, n = w.shape
    w = f64(np.asarray(w, np.float32).astype(ml_dtypes.bfloat16)).reshape(k // 32, 32, n)
    amax = np.abs(w).max(1)
    if fmt == "e4m3":
        byte = np.frexp(amax)[1] - 1 + 127 - 7
    else:
        mant, ex = np.frexp(amax / 6.0)
        byte = np.where(mant > 0.5, ex, ex - 1) + 127
    byte = np.clip(np.where(amax > 0, byte, 1), 1, 254)
    scaled = (w * np.exp2(127.0 - byte)[:, None, :]).reshape(k, n).astype(np.float32)
    by_word = np.ascontiguousarray(scaled.reshape(k // 512, 128, 4, n).transpose(0, 1, 3, 2))
    if fmt == "e4m3":
        words = by_word.astype(ml_dtypes.float8_e4m3fn).view(np.uint8)
    else:
        c = by_word.astype(ml_dtypes.float4_e2m1fn).view(np.uint8) & 0xF
        words = (c[..., 0::2] | (c[..., 1::2] << 4)).reshape(k // 512, 128, 2 * n)
    return np.ascontiguousarray(words), np.ascontiguousarray(byte.astype(np.uint8).reshape(k // 512, 16, n))


def unpack_weight(words, scales, fmt):
    g, _, n = scales.shape
    words = np.ascontiguousarray(words).reshape(g, 128, n, -1)
    if fmt == "e4m3":
        vals = words.view(ml_dtypes.float8_e4m3fn).astype(np.float64)
    else:
        nib = np.empty((g, 128, n, 4), np.uint8)
        nib[..., 0::2] = words & 0xF
        nib[..., 1::2] = words >> 4
        vals = E2M1[nib]
    vals = vals * np.repeat(np.exp2(scales.astype(np.float64) - 127.0), 8, axis=1)[..., None]
    return vals.transpose(0, 1, 3, 2).reshape(g * 512, n)


def gelu(v):
    return 0.5 * v * (1.0 + np.tanh(np.sqrt(2.0 / np.pi) * (v + 0.044715 * v**3)))


K, H, N, T, S = 512, 1024, 512, 4096, 1024

def setup_inputs():
    n = np.random.standard_normal
    s = mx_kscale(K)[:, None]
    u = mx_kscale(H)[:, None]
    tab_words, tab_scales = pack_weight(n((K, T)) * s, "e2m1")
    w1 = (n((K, H)) / np.sqrt(K) / s).astype(np.float32)
    w8_words, w8_scales = pack_weight(n((K, H)) / np.sqrt(K) / s, "e4m3")
    w4_words, w4_scales = pack_weight(n((H, N)) / np.sqrt(H) / u, "e2m1")
    gain = (2.0 * np.exp(0.3 * n(H)) * u[:, 0]).astype(np.float32)
    return {
        "tab_words": tab_words, "tab_scales": tab_scales,
        "offs": striped(np.random.permutation(T)[:S]),
        "offs2": striped(np.random.permutation(T)[:S]),
        "w1": w1, "w8_words": w8_words, "w8_scales": w8_scales,
        "w4_words": w4_words, "w4_scales": w4_scales, "gain": gain,
    }

def reference(tab_words, tab_scales, offs, offs2, w1, w8_words, w8_scales, w4_words, w4_scales, gain):
    TW = unpack_weight(tab_words, tab_scales, "e2m1")
    v = TW[:, unstriped(offs)]
    v2 = TW[:, unstriped(offs2)]
    w8 = unpack_weight(w8_words, w8_scales, "e4m3")
    w4 = unpack_weight(w4_words, w4_scales, "e2m1")
    a = mxq(f64(w1), 0, "e4m3").T @ v
    b = w8.T @ v2
    q = np.square(b)
    resp = q / (1.0 + q)
    act = 1.0 / (1.0 + np.exp(-a))
    h = f64(gain)[:, None] * (resp * act)
    return w4.T @ mxq(h, 0, "e4m3")

@@ -1,0 +1,229 @@
+from contextlib import ExitStack
+
+import concourse.mybir as mybir
+
+K, H, N, T, S = 512, 1024, 512, 4096, 1024
+FLOPS = 2 * K * H * S * 2 + 2 * H * N * S
+
+F32 = mybir.dt.float32
+BF16 = mybir.dt.bfloat16
+I32 = mybir.dt.int32
+U16 = mybir.dt.uint16
+U8 = mybir.dt.uint8
+FP8X4 = mybir.dt.float8_e4m3fn_x4
+FP4X4 = mybir.dt.float4_e2m1fn_x4
+ACT = mybir.ActivationFunctionType
+ALU = mybir.AluOpType
+
+P = 128
+W = 512
+LN_FLOOR = 2.0 ** -60
+UNITS = [(jh, a) for jh in range(2) for a in range(2)]
+ABS_ON_VECTOR = {(1, 2), (2, 2), (3, 2), (0, 3), (2, 3)}
+TAIL = 256
+
+
+def tile_list_trophic_link_energy_kernel(
+    tc, tab_words, tab_scales, offs, offs2, w1, w8_words, w8_scales, w4_words, w4_scales, gain, out
+):
+    nc = tc.nc
+    with ExitStack() as ctx:
+        keep = ctx.enter_context(tc.tile_pool(name="keep", bufs=1))
+        ring = ctx.enter_context(tc.tile_pool(name="ring", bufs=2))
+        psum_in = ctx.enter_context(tc.psum_pool(name="psum_in", bufs=5))
+        psum_out = ctx.enter_context(tc.psum_pool(name="psum_out", bufs=3))
+
+        list_pred = keep.tile([P, S // 16], U16, name="list_pred")
+        list_prey = keep.tile([P, S // 16], U16, name="list_prey")
+        tabw = keep.tile([P, T], U16, name="tabw", align_bytes=64)
+        tabs = keep.tile([P, T], U8, name="tabs", align_bytes=64)
+        w8s_raw = keep.tile([P, H], U8, name="w8s_raw", tag="early_a", align_bytes=64)
+        w8w_raw = keep.tile([P, H], I32, name="w8w_raw", tag="early_b", align_bytes=64)
+        gains = keep.tile([P, 2, 4], F32, name="gains")
+        ones = keep.tile([P, 1], F32, name="ones")
+        warm = keep.tile([P, 1], F32, name="warm")
+
+        nc.vector.memset(tabs[:].bitcast(I32), 0)
+        nc.vector.memset(w8s_raw[:].bitcast(I32), 0)
+        nc.vector.memset(ones[:], 1.0)
+
+        nc.sync.dma_start(list_prey[:], offs2)
+        nc.sync.dma_start(tabw[:].bitcast(I32), tab_words[0].bitcast(I32))
+        nc.sync.dma_start(w8w_raw[:], w8_words[0].rearrange("p n t -> p (n t)").bitcast(I32))
+        nc.sync.dma_start(list_pred[:], offs)
+        for q in range(4):
+            nc.scalar.dma_start(tabs[32 * q : 32 * q + 4, :].bitcast(I32), tab_scales[0, 4 * q : 4 * q + 4, :].bitcast(I32))
+        for q in range(4):
+            (nc.scalar if q < 2 else nc.gpsimd).dma_start(w8s_raw[32 * q : 32 * q + 4, :].bitcast(I32), w8_scales[0, 4 * q : 4 * q + 4, :].bitcast(I32))
+        nc.gpsimd.dma_start(gains[:], gain.rearrange("(a p t) -> p a t", a=2, t=4))
+        nc.scalar.activation(warm[:], ones[:], ACT.Ln)
+
+        def gather(window, offsets, jh, dtype, name):
+            picked = keep.tile([P, W], dtype, name=name, align_bytes=64)
+            nc.vector.tensor_copy(picked[:], window[:].indirect(offsets[:, jh * (W // 16) : (jh + 1) * (W // 16)]))
+            return picked
+
+        prey_s, prey_w, pred_s, pred_w = {}, {}, {}, {}
+        prey_s[0] = gather(tabs, list_prey, 0, U8, "prey_s0")
+        w8s = keep.tile([P, H], U8, name="w8s", align_bytes=64)
+        nc.vector.tensor_copy(
+            w8s[:].rearrange("p (a t m) -> p a m t", a=2, t=4), w8s_raw[:].rearrange("p (a m t) -> p a m t", a=2, t=4)
+        )
+        prey_w[0] = gather(tabw, list_prey, 0, U16, "prey_w0")
+        w8w = []
+        for a in range(2):
+            w8w.append(keep.tile([P, W], I32, name=f"w8w{a}", align_bytes=64))
+            nc.vector.tensor_copy(
+                w8w[a][:].rearrange("p (t m) -> p m t", t=4),
+                w8w_raw[:, a * W : (a + 1) * W].rearrange("p (m t) -> p m t", t=4),
+            )
+        prey_s[1] = gather(tabs, list_prey, 1, U8, "prey_s1")
+        prey_w[1] = gather(tabw, list_prey, 1, U16, "prey_w1")
+
+        w1_rows = w1.rearrange("(p j) c -> p j c", j=4)
+        w1_raw = []
+        for a in range(2):
+            w1_raw.append(keep.tile([P, 4, W], F32, name=f"w1_raw{a}", tag=("early_a", "early_b")[a], align_bytes=64))
+            nc.sync.dma_start(w1_raw[a][:], w1_rows[:, :, a * W : (a + 1) * W])
+
+        logs = keep.tile([P, 4, 4, W], F32, name="logs")
+        gates = keep.tile([P, 4, W], F32, name="gates")
+
+        def prey_magnitude(u, t, dest):
+            jh, a = UNITS[u]
+            bank = psum_in.tile([P, W], F32, name="bank_in")
+            nc.tensor.matmul_mx(
+                bank[:],
+                lhsT=w8w[a][:, t * P : (t + 1) * P].bitcast(FP8X4),
+                lhsT_scale=w8s[:, a * W + t * P : a * W + (t + 1) * P],
+                rhs=prey_w[jh][:].bitcast(FP4X4),
+                rhs_scale=prey_s[jh][:],
+                start=True,
+                stop=True,
+            )
+            if (u, t) in ABS_ON_VECTOR:
+                negated = ring.tile([P, W], F32, name="negated")
+                nc.vector.tensor_scalar(negated[:], bank[:], -1.0, None, ALU.mult)
+                nc.vector.tensor_tensor(dest, bank[:], negated[:], ALU.max)
+            else:
+                nc.scalar.activation(dest, bank[:], ACT.Abs)
+
+        w1w, w1s, w1_grouped = [], [], []
+
+        def round_w1(a):
+            grouped = ring.tile([P, 4 * W], BF16, name="w1_grouped", align_bytes=64)
+            nc.vector.tensor_copy(
+                grouped[:].rearrange("p (t m j) -> p m j t", t=4, j=4),
+                w1_raw[a][:].rearrange("p j (m t) -> p m j t", t=4),
+            )
+            w1_grouped.append(grouped)
+
+        def quantize_w1(a):
+            w1w.append(keep.tile([P, W], I32, name=f"w1w{a}", align_bytes=64))
+            w1s.append(keep.tile([P, W], U8, name=f"w1s{a}", align_bytes=64))
+            nc.vector.quantize_mx(w1w[a][:].bitcast(FP8X4), w1s[a][:], w1_grouped[a][:])
+
+        for u in range(4):
+            mags = ring.tile([P, 3, W], F32, name="mags")
+            for t in range(3):
+                prey_magnitude(u, t, mags[:, t, :])
+            nc.scalar.activation(logs[:, u, 0:3, :], mags[:], ACT.Ln, bias=LN_FLOOR)
+            if u == 1:
+                pred_s[0] = gather(tabs, list_pred, 0, U8, "pred_s0")
+            if u == 2:
+                round_w1(0)
+                pred_w[0] = gather(tabw, list_pred, 0, U16, "pred_w0")
+            if u == 3:
+                quantize_w1(0)
+        for u in range(4):
+            prey_magnitude(u, 3, gates[:, u, :])
+        nc.scalar.activation(logs[:, :, 3, :], gates[:], ACT.Ln, bias=LN_FLOOR)
+        round_w1(1)
+        pred_s[1] = gather(tabs, list_pred, 1, U8, "pred_s1")
+        quantize_w1(1)
+        pred_w[1] = gather(tabw, list_pred, 1, U16, "pred_w1")
+
+        w4w = keep.tile([P, 2, N], U16, name="w4w", tag="early_a", align_bytes=64)
+        nc.sync.dma_start(w4w[:].bitcast(I32), w4_words.rearrange("a p c -> p a c").bitcast(I32))
+        w4s = keep.tile([P, 2, N], U8, name="w4s", tag="early_b", align_bytes=64)
+        nc.gpsimd.memset(w4s[:].bitcast(I32), 0)
+        for q in range(4):
+            nc.sync.dma_start(
+                w4s[32 * q : 32 * q + 4, :, :].bitcast(I32),
+                w4_scales[:, 4 * q : 4 * q + 4, :].rearrange("a r c -> r a c").bitcast(I32),
+            )
+
+        hw = [keep.tile([P, W], I32, name=f"hw{u}", align_bytes=64) for u in range(4)]
+        hs = [keep.tile([P, W], U8, name=f"hs{u}", align_bytes=64) for u in range(4)]
+
+        def predator_gate(u, t):
+            jh, a = UNITS[u]
+            bank = psum_in.tile([P, W], F32, name="bank_in")
+            nc.tensor.matmul_mx(
+                bank[:],
+                lhsT=w1w[a][:, t * P : (t + 1) * P].bitcast(FP8X4),
+                lhsT_scale=w1s[a][:, t * P : (t + 1) * P],
+                rhs=pred_w[jh][:].bitcast(FP4X4),
+                rhs_scale=pred_s[jh][:],
+                start=True,
+                stop=True,
+            )
+            nc.scalar.activation(gates[:, t, :], bank[:], ACT.Sigmoid)
+
+        def make_h(u, c0, width):
+            a = UNITS[u][1]
+            cols = slice(c0, c0 + width)
+            resp = ring.tile([P, 4, width], F32, name="resp")
+            nc.scalar.activation(resp[:], logs[:, u, :, cols], ACT.Sigmoid, scale=2.0)
+            if c0 == 0:
+                for t in range(4):
+                    predator_gate(u, t)
+            planes = ring.tile([P, 4, width], BF16, name="planes")
+            for t in range(4):
+                nc.vector.scalar_tensor_tensor(
+                    planes[:, t, :], resp[:, t, :], gains[:, a, t : t + 1], gates[:, t, cols], ALU.mult, ALU.mult
+                )
+            woven = ring.tile([P, 4 * width], BF16, name="woven", align_bytes=64)
+            nc.vector.tensor_copy(
+                woven[:].rearrange("p (c i t) -> p c t i", i=4, t=4),
+                planes[:].rearrange("p t (c i) -> p c t i", i=4),
+            )
+            nc.vector.quantize_mx(hw[u][:, cols].bitcast(FP8X4), hs[u][:, cols], woven[:])
+
+        def convert(dest, nt, jh, cols):
+            for a in range(2):
+                u = 2 * jh + a
+                nc.tensor.matmul_mx(
+                    dest,
+                    lhsT=w4w[:, a, nt * P : (nt + 1) * P].bitcast(FP4X4),
+                    lhsT_scale=w4s[:, a, nt * P : (nt + 1) * P],
+                    rhs=hw[u][:, cols].bitcast(FP8X4),
+                    rhs_scale=hs[u][:, cols],
+                    start=(a == 0),
+                    stop=(a == 1),
+                )
+
+        def leave(bank, dest, on_scalar, name):
+            result = keep.tile([P, W], F32, name=name)
+            if on_scalar:
+                nc.scalar.copy(result[:], bank[:])
+            else:
+                nc.vector.tensor_copy(result[:], bank[:])
+            nc.sync.dma_start(dest, result[:].rearrange("p (n j) -> p n j", n=dest.shape[1]))
+
+        out_rows = out.rearrange("(n p) j -> p n j", p=P)
+        make_h(0, 0, W)
+        make_h(1, 0, W)
+        make_h(2, 0, W)
+        for nt in range(4):
+            bank = psum_out.tile([P, W], F32, name="bank_out")
+            convert(bank[:], nt, 0, slice(0, W))
+            leave(bank, out_rows[:, nt : nt + 1, 0:W], nt % 2 == 1, f"result0_{nt}")
+        for c0 in range(0, W, TAIL):
+            make_h(3, c0, TAIL)
+            for pair in range(2):
+                bank = psum_out.tile([P, W], F32, name="bank_out")
+                for i in range(2):
+                    for j0 in range(0, TAIL, P):
+                        convert(bank[:, i * TAIL + j0 : i * TAIL + j0 + P], 2 * pair + i, 1, slice(c0 + j0, c0 + j0 + P))
+                leave(bank, out_rows[:, 2 * pair : 2 * pair + 2, W + c0 : W + c0 + TAIL], pair == 0, f"result1_{c0}_{pair}")

@@ -19,8 +19,7 @@ P = 128
 W = 512
 LN_FLOOR = 2.0 ** -60
 UNITS = [(jh, a) for jh in range(2) for a in range(2)]
-ABS_ON_VECTOR = {(1, 2), (2, 2), (3, 2), (0, 3), (2, 3)}
-TAIL = 256
+TAIL = [(0, 256), (256, 128), (384, 128)]
 
 
 def tile_list_trophic_link_energy_kernel(
@@ -30,55 +29,67 @@ def tile_list_trophic_link_energy_kernel(
     with ExitStack() as ctx:
         keep = ctx.enter_context(tc.tile_pool(name="keep", bufs=1))
         ring = ctx.enter_context(tc.tile_pool(name="ring", bufs=2))
-        psum_in = ctx.enter_context(tc.psum_pool(name="psum_in", bufs=5))
-        psum_out = ctx.enter_context(tc.psum_pool(name="psum_out", bufs=3))
+        ring3 = ctx.enter_context(tc.tile_pool(name="ring3", bufs=4))
+        psum = ctx.enter_context(tc.psum_pool(name="psum", bufs=6))
+        psum_v = ctx.enter_context(tc.psum_pool(name="psum_v", bufs=2))
 
         list_pred = keep.tile([P, S // 16], U16, name="list_pred")
         list_prey = keep.tile([P, S // 16], U16, name="list_prey")
         tabw = keep.tile([P, T], U16, name="tabw", align_bytes=64)
         tabs = keep.tile([P, T], U8, name="tabs", align_bytes=64)
         w8s_raw = keep.tile([P, H], U8, name="w8s_raw", tag="early_a", align_bytes=64)
-        w8w_raw = keep.tile([P, H], I32, name="w8w_raw", tag="early_b", align_bytes=64)
-        gains = keep.tile([P, 2, 4], F32, name="gains")
         ones = keep.tile([P, 1], F32, name="ones")
         warm = keep.tile([P, 1], F32, name="warm")
 
-        nc.vector.memset(tabs[:].bitcast(I32), 0)
+        nc.gpsimd.memset(tabs[:].bitcast(I32), 0)
         nc.vector.memset(w8s_raw[:].bitcast(I32), 0)
         nc.vector.memset(ones[:], 1.0)
 
+        w8_rows = w8_words[0].rearrange("p n t -> p (n t)").bitcast(I32)
+
+        def load_w8(a):
+            raw = keep.tile([P, W], I32, name=f"w8w_raw{a}", tag="early_b", align_bytes=64)
+            nc.sync.dma_start(raw[:], w8_rows[:, a * W : (a + 1) * W])
+            return raw
+
+        def reorder_w8(a, raw):
+            words = keep.tile([P, W], I32, name=f"w8w{a}", align_bytes=64)
+            nc.vector.tensor_copy(words[:].rearrange("p (t m) -> p m t", t=4), raw[:].rearrange("p (m t) -> p m t", t=4))
+            return words
+
         nc.sync.dma_start(list_prey[:], offs2)
-        nc.sync.dma_start(tabw[:].bitcast(I32), tab_words[0].bitcast(I32))
-        nc.sync.dma_start(w8w_raw[:], w8_words[0].rearrange("p n t -> p (n t)").bitcast(I32))
         nc.sync.dma_start(list_pred[:], offs)
+        nc.sync.dma_start(tabw[:].bitcast(I32), tab_words[0].bitcast(I32))
+        w8w_raw0 = load_w8(0)
+        for q in range(4):
+            (nc.scalar if q < 3 else nc.gpsimd).dma_start(w8s_raw[32 * q : 32 * q + 4, :].bitcast(I32), w8_scales[0, 4 * q : 4 * q + 4, :].bitcast(I32))
         for q in range(4):
             nc.scalar.dma_start(tabs[32 * q : 32 * q + 4, :].bitcast(I32), tab_scales[0, 4 * q : 4 * q + 4, :].bitcast(I32))
-        for q in range(4):
-            (nc.scalar if q < 2 else nc.gpsimd).dma_start(w8s_raw[32 * q : 32 * q + 4, :].bitcast(I32), w8_scales[0, 4 * q : 4 * q + 4, :].bitcast(I32))
-        nc.gpsimd.dma_start(gains[:], gain.rearrange("(a p t) -> p a t", a=2, t=4))
         nc.scalar.activation(warm[:], ones[:], ACT.Ln)
+        gains = keep.tile([P, 2, 4], F32, name="gains", tag="ones")
+        nc.sync.dma_start(gains[:], gain.rearrange("(a p t) -> p a t", a=2, t=4))
 
-        def gather(window, offsets, jh, dtype, name):
-            picked = keep.tile([P, W], dtype, name=name, align_bytes=64)
-            nc.vector.tensor_copy(picked[:], window[:].indirect(offsets[:, jh * (W // 16) : (jh + 1) * (W // 16)]))
+        def gather(window, offsets, first, count, dtype, name, tag):
+            picked = keep.tile([P, count], dtype, name=name, tag=tag, align_bytes=64)
+            nc.vector.tensor_copy(picked[:], window[:].indirect(offsets[:, first // 16 : (first + count) // 16]))
             return picked
 
-        prey_s, prey_w, pred_s, pred_w = {}, {}, {}, {}
-        prey_s[0] = gather(tabs, list_prey, 0, U8, "prey_s0")
-        w8s = keep.tile([P, H], U8, name="w8s", align_bytes=64)
-        nc.vector.tensor_copy(
-            w8s[:].rearrange("p (a t m) -> p a m t", a=2, t=4), w8s_raw[:].rearrange("p (a m t) -> p a m t", a=2, t=4)
-        )
-        prey_w[0] = gather(tabw, list_prey, 0, U16, "prey_w0")
-        w8w = []
-        for a in range(2):
-            w8w.append(keep.tile([P, W], I32, name=f"w8w{a}", align_bytes=64))
+        prey_s, prey_w = {}, {}
+        def reorder_w8_scales(a):
+            scales = keep.tile([P, W], U8, name=f"w8s{a}", align_bytes=64)
             nc.vector.tensor_copy(
-                w8w[a][:].rearrange("p (t m) -> p m t", t=4),
-                w8w_raw[:, a * W : (a + 1) * W].rearrange("p (m t) -> p m t", t=4),
+                scales[:].rearrange("p (t m) -> p m t", t=4), w8s_raw[:, a * W : (a + 1) * W].rearrange("p (m t) -> p m t", t=4)
             )
-        prey_s[1] = gather(tabs, list_prey, 1, U8, "prey_s1")
-        prey_w[1] = gather(tabw, list_prey, 1, U16, "prey_w1")
+            return scales
+
+        w8s = [reorder_w8_scales(0)]
+        w8w = [reorder_w8(0, w8w_raw0)]
+        prey_w[0] = gather(tabw, list_prey, 0, W, U16, "prey_w0", "w0")
+        prey_s[0] = gather(tabs, list_prey, 0, W, U8, "prey_s0", "s0")
+        w8s.append(reorder_w8_scales(1))
+        w8w.append(reorder_w8(1, load_w8(1)))
+        prey_s[1] = gather(tabs, list_prey, W, W, U8, "prey_s1", "s1")
+        prey_w[1] = gather(tabw, list_prey, W, W, U16, "prey_w1", "w1")
 
         w1_rows = w1.rearrange("(p j) c -> p j c", j=4)
         w1_raw = []
@@ -89,20 +100,20 @@ def tile_list_trophic_link_energy_kernel(
         logs = keep.tile([P, 4, 4, W], F32, name="logs")
         gates = keep.tile([P, 4, W], F32, name="gates")
 
-        def prey_magnitude(u, t, dest):
+        def prey_magnitude(u, t, dest, on_vector):
             jh, a = UNITS[u]
-            bank = psum_in.tile([P, W], F32, name="bank_in")
+            bank = (psum_v if on_vector else psum).tile([P, W], F32, name="bank")
             nc.tensor.matmul_mx(
                 bank[:],
                 lhsT=w8w[a][:, t * P : (t + 1) * P].bitcast(FP8X4),
-                lhsT_scale=w8s[:, a * W + t * P : a * W + (t + 1) * P],
+                lhsT_scale=w8s[a][:, t * P : (t + 1) * P],
                 rhs=prey_w[jh][:].bitcast(FP4X4),
                 rhs_scale=prey_s[jh][:],
                 start=True,
                 stop=True,
             )
-            if (u, t) in ABS_ON_VECTOR:
-                negated = ring.tile([P, W], F32, name="negated")
+            if on_vector:
+                negated = ring.tile([P, W], F32, name="negated", align_bytes=64)
                 nc.vector.tensor_scalar(negated[:], bank[:], -1.0, None, ALU.mult)
                 nc.vector.tensor_tensor(dest, bank[:], negated[:], ALU.max)
             else:
@@ -111,7 +122,7 @@ def tile_list_trophic_link_energy_kernel(
         w1w, w1s, w1_grouped = [], [], []
 
         def round_w1(a):
-            grouped = ring.tile([P, 4 * W], BF16, name="w1_grouped", align_bytes=64)
+            grouped = ring.tile([P, 4 * W], BF16, name="w1_grouped", tag=("w1_grouped", "negated")[a], align_bytes=64)
             nc.vector.tensor_copy(
                 grouped[:].rearrange("p (t m j) -> p m j t", t=4, j=4),
                 w1_raw[a][:].rearrange("p j (m t) -> p m j t", t=4),
@@ -123,25 +134,20 @@ def tile_list_trophic_link_energy_kernel(
             w1s.append(keep.tile([P, W], U8, name=f"w1s{a}", align_bytes=64))
             nc.vector.quantize_mx(w1w[a][:].bitcast(FP8X4), w1s[a][:], w1_grouped[a][:])
 
+        round_w1(0)
+        quantize_w1(0)
         for u in range(4):
-            mags = ring.tile([P, 3, W], F32, name="mags")
+            mags = ring3.tile([P, 3, W], F32, name="mags")
             for t in range(3):
-                prey_magnitude(u, t, mags[:, t, :])
+                prey_magnitude(u, t, mags[:, t, :], u == 3)
             nc.scalar.activation(logs[:, u, 0:3, :], mags[:], ACT.Ln, bias=LN_FLOOR)
-            if u == 1:
-                pred_s[0] = gather(tabs, list_pred, 0, U8, "pred_s0")
-            if u == 2:
-                round_w1(0)
-                pred_w[0] = gather(tabw, list_pred, 0, U16, "pred_w0")
-            if u == 3:
-                quantize_w1(0)
         for u in range(4):
-            prey_magnitude(u, 3, gates[:, u, :])
+            prey_magnitude(u, 3, gates[:, u, :], True)
         nc.scalar.activation(logs[:, :, 3, :], gates[:], ACT.Ln, bias=LN_FLOOR)
+        pred_s = gather(tabs, list_pred, 0, S, U8, "pred_s", "s1")
+        pred_w = gather(tabw, list_pred, 0, S, U16, "pred_w", "w1")
         round_w1(1)
-        pred_s[1] = gather(tabs, list_pred, 1, U8, "pred_s1")
         quantize_w1(1)
-        pred_w[1] = gather(tabw, list_pred, 1, U16, "pred_w1")
 
         w4w = keep.tile([P, 2, N], U16, name="w4w", tag="early_a", align_bytes=64)
         nc.sync.dma_start(w4w[:].bitcast(I32), w4_words.rearrange("a p c -> p a c").bitcast(I32))
@@ -156,30 +162,28 @@ def tile_list_trophic_link_energy_kernel(
         hw = [keep.tile([P, W], I32, name=f"hw{u}", align_bytes=64) for u in range(4)]
         hs = [keep.tile([P, W], U8, name=f"hs{u}", align_bytes=64) for u in range(4)]
 
-        def predator_gate(u, t):
+        def predator_product(u, t):
             jh, a = UNITS[u]
-            bank = psum_in.tile([P, W], F32, name="bank_in")
+            bank = psum.tile([P, W], F32, name="bank")
             nc.tensor.matmul_mx(
                 bank[:],
                 lhsT=w1w[a][:, t * P : (t + 1) * P].bitcast(FP8X4),
                 lhsT_scale=w1s[a][:, t * P : (t + 1) * P],
-                rhs=pred_w[jh][:].bitcast(FP4X4),
-                rhs_scale=pred_s[jh][:],
+                rhs=pred_w[:, jh * W : (jh + 1) * W].bitcast(FP4X4),
+                rhs_scale=pred_s[:, jh * W : (jh + 1) * W],
                 start=True,
                 stop=True,
             )
-            nc.scalar.activation(gates[:, t, :], bank[:], ACT.Sigmoid)
+            return bank
 
-        def make_h(u, c0, width):
+        def make_h(u, banks, c0, width):
             a = UNITS[u][1]
             cols = slice(c0, c0 + width)
             resp = ring.tile([P, 4, width], F32, name="resp")
             nc.scalar.activation(resp[:], logs[:, u, :, cols], ACT.Sigmoid, scale=2.0)
-            if c0 == 0:
-                for t in range(4):
-                    predator_gate(u, t)
             planes = ring.tile([P, 4, width], BF16, name="planes")
             for t in range(4):
+                nc.scalar.activation(gates[:, t, cols], banks[t][:, cols], ACT.Sigmoid)
                 nc.vector.scalar_tensor_tensor(
                     planes[:, t, :], resp[:, t, :], gains[:, a, t : t + 1], gates[:, t, cols], ALU.mult, ALU.mult
                 )
@@ -190,18 +194,17 @@ def tile_list_trophic_link_energy_kernel(
             )
             nc.vector.quantize_mx(hw[u][:, cols].bitcast(FP8X4), hs[u][:, cols], woven[:])
 
-        def convert(dest, nt, jh, cols):
-            for a in range(2):
-                u = 2 * jh + a
-                nc.tensor.matmul_mx(
-                    dest,
-                    lhsT=w4w[:, a, nt * P : (nt + 1) * P].bitcast(FP4X4),
-                    lhsT_scale=w4s[:, a, nt * P : (nt + 1) * P],
-                    rhs=hw[u][:, cols].bitcast(FP8X4),
-                    rhs_scale=hs[u][:, cols],
-                    start=(a == 0),
-                    stop=(a == 1),
-                )
+        def convert(dest, nt, u, cols, start, stop):
+            a = UNITS[u][1]
+            nc.tensor.matmul_mx(
+                dest,
+                lhsT=w4w[:, a, nt * P : (nt + 1) * P].bitcast(FP4X4),
+                lhsT_scale=w4s[:, a, nt * P : (nt + 1) * P],
+                rhs=hw[u][:, cols].bitcast(FP8X4),
+                rhs_scale=hs[u][:, cols],
+                start=start,
+                stop=stop,
+            )
 
         def leave(bank, dest, on_scalar, name):
             result = keep.tile([P, W], F32, name=name)
@@ -212,18 +215,37 @@ def tile_list_trophic_link_energy_kernel(
             nc.sync.dma_start(dest, result[:].rearrange("p (n j) -> p n j", n=dest.shape[1]))
 
         out_rows = out.rearrange("(n p) j -> p n j", p=P)
-        make_h(0, 0, W)
-        make_h(1, 0, W)
-        make_h(2, 0, W)
+        for u in range(3):
+            make_h(u, [predator_product(u, t) for t in range(4)], 0, W)
         for nt in range(4):
-            bank = psum_out.tile([P, W], F32, name="bank_out")
-            convert(bank[:], nt, 0, slice(0, W))
+            bank = psum.tile([P, W], F32, name="bank")
+            convert(bank[:], nt, 0, slice(0, W), True, False)
+            convert(bank[:], nt, 1, slice(0, W), False, True)
             leave(bank, out_rows[:, nt : nt + 1, 0:W], nt % 2 == 1, f"result0_{nt}")
-        for c0 in range(0, W, TAIL):
-            make_h(3, c0, TAIL)
-            for pair in range(2):
-                bank = psum_out.tile([P, W], F32, name="bank_out")
-                for i in range(2):
-                    for j0 in range(0, TAIL, P):
-                        convert(bank[:, i * TAIL + j0 : i * TAIL + j0 + P], 2 * pair + i, 1, slice(c0 + j0, c0 + j0 + P))
-                leave(bank, out_rows[:, 2 * pair : 2 * pair + 2, W + c0 : W + c0 + TAIL], pair == 0, f"result1_{c0}_{pair}")
+
+        last_banks = [predator_product(3, t) for t in range(4)]
+        sums = []
+        for c0, width in TAIL:
+            per_bank = W // width
+            for n0 in range(0, 4, per_bank):
+                bank = (psum_v if width == 256 else psum).tile([P, W], F32, name="bank")
+                pieces = [(i, j0) for i in range(per_bank) for j0 in range(0, width, P)]
+                sums.append((bank, c0, width, n0, per_bank, pieces))
+
+        def convert_pieces(u, entry):
+            bank, c0, width, n0, per_bank, pieces = entry
+            for k, (i, j0) in enumerate(pieces):
+                convert(
+                    bank[:, i * width + j0 : i * width + j0 + P], n0 + i, u, slice(c0 + j0, c0 + j0 + P),
+                    u == 2 and k == 0, u == 3 and k == len(pieces) - 1,
+                )
+
+        for entry in sums:
+            convert_pieces(2, entry)
+        for c0, width in TAIL:
+            make_h(3, last_banks, c0, width)
+            for entry in sums:
+                if entry[1] == c0:
+                    convert_pieces(3, entry)
+        for k, (bank, c0, width, n0, per_bank, pieces) in enumerate(sums):
+            leave(bank, out_rows[:, n0 : n0 + per_bank, W + c0 : W + c0 + width], k < len(sums) - 1, f"result1_{k}")

@@ -41,8 +41,8 @@ def tile_list_trophic_link_energy_kernel(
         ones = keep.tile([P, 1], F32, name="ones")
         warm = keep.tile([P, 1], F32, name="warm")
 
-        nc.gpsimd.memset(tabs[:].bitcast(I32), 0)
-        nc.vector.memset(w8s_raw[:].bitcast(I32), 0)
+        nc.gpsimd.memset(w8s_raw[:].bitcast(I32), 0)
+        nc.vector.memset(tabs[:].bitcast(I32), 0)
         nc.vector.memset(ones[:], 1.0)
 
         w8_rows = w8_words[0].rearrange("p n t -> p (n t)").bitcast(I32)
@@ -59,15 +59,15 @@ def tile_list_trophic_link_energy_kernel(
 
         nc.sync.dma_start(list_prey[:], offs2)
         nc.sync.dma_start(list_pred[:], offs)
-        nc.sync.dma_start(tabw[:].bitcast(I32), tab_words[0].bitcast(I32))
         w8w_raw0 = load_w8(0)
+        nc.sync.dma_start(tabw[:].bitcast(I32), tab_words[0].bitcast(I32))
         for q in range(4):
-            (nc.scalar if q < 3 else nc.gpsimd).dma_start(w8s_raw[32 * q : 32 * q + 4, :].bitcast(I32), w8_scales[0, 4 * q : 4 * q + 4, :].bitcast(I32))
+            (nc.scalar if q < 2 else nc.gpsimd).dma_start(w8s_raw[32 * q : 32 * q + 4, :].bitcast(I32), w8_scales[0, 4 * q : 4 * q + 4, :].bitcast(I32))
         for q in range(4):
-            nc.scalar.dma_start(tabs[32 * q : 32 * q + 4, :].bitcast(I32), tab_scales[0, 4 * q : 4 * q + 4, :].bitcast(I32))
+            nc.sync.dma_start(tabs[32 * q : 32 * q + 4, :].bitcast(I32), tab_scales[0, 4 * q : 4 * q + 4, :].bitcast(I32))
         nc.scalar.activation(warm[:], ones[:], ACT.Ln)
         gains = keep.tile([P, 2, 4], F32, name="gains", tag="ones")
-        nc.sync.dma_start(gains[:], gain.rearrange("(a p t) -> p a t", a=2, t=4))
+        nc.gpsimd.dma_start(gains[:], gain.rearrange("(a p t) -> p a t", a=2, t=4))
 
         def gather(window, offsets, first, count, dtype, name, tag):
             picked = keep.tile([P, count], dtype, name=name, tag=tag, align_bytes=64)
@@ -89,13 +89,9 @@ def tile_list_trophic_link_energy_kernel(
         w8s.append(reorder_w8_scales(1))
         w8w.append(reorder_w8(1, load_w8(1)))
         prey_s[1] = gather(tabs, list_prey, W, W, U8, "prey_s1", "s1")
-        prey_w[1] = gather(tabw, list_prey, W, W, U16, "prey_w1", "w1")
+        prey_w[1] = gather(tabw, list_prey, W, W, U16, "prey_w1", "early_b")
 
         w1_rows = w1.rearrange("(p j) c -> p j c", j=4)
-        w1_raw = []
-        for a in range(2):
-            w1_raw.append(keep.tile([P, 4, W], F32, name=f"w1_raw{a}", tag=("early_a", "early_b")[a], align_bytes=64))
-            nc.sync.dma_start(w1_raw[a][:], w1_rows[:, :, a * W : (a + 1) * W])
 
         logs = keep.tile([P, 4, 4, W], F32, name="logs")
         gates = keep.tile([P, 4, W], F32, name="gates")
@@ -121,11 +117,16 @@ def tile_list_trophic_link_energy_kernel(
 
         w1w, w1s, w1_grouped = [], [], []
 
-        def round_w1(a):
+        def load_w1(a):
+            raw = keep.tile([P, 4, W], F32, name=f"w1_raw{a}", tag="early_a", align_bytes=64)
+            nc.sync.dma_start(raw[:], w1_rows[:, :, a * W : (a + 1) * W])
+            return raw
+
+        def round_w1(a, raw):
             grouped = ring.tile([P, 4 * W], BF16, name="w1_grouped", tag=("w1_grouped", "negated")[a], align_bytes=64)
             nc.vector.tensor_copy(
                 grouped[:].rearrange("p (t m j) -> p m j t", t=4, j=4),
-                w1_raw[a][:].rearrange("p j (m t) -> p m j t", t=4),
+                raw[:].rearrange("p j (m t) -> p m j t", t=4),
             )
             w1_grouped.append(grouped)
 
@@ -134,24 +135,28 @@ def tile_list_trophic_link_energy_kernel(
             w1s.append(keep.tile([P, W], U8, name=f"w1s{a}", align_bytes=64))
             nc.vector.quantize_mx(w1w[a][:].bitcast(FP8X4), w1s[a][:], w1_grouped[a][:])
 
-        round_w1(0)
+        round_w1(0, load_w1(0))
         quantize_w1(0)
+        w1_raw1 = load_w1(1)
+        mags = []
         for u in range(4):
-            mags = ring3.tile([P, 3, W], F32, name="mags")
+            mags.append(ring3.tile([P, 3, W], F32, name="mags"))
             for t in range(3):
-                prey_magnitude(u, t, mags[:, t, :], u == 3)
-            nc.scalar.activation(logs[:, u, 0:3, :], mags[:], ACT.Ln, bias=LN_FLOOR)
+                prey_magnitude(u, t, mags[u][:, t, :], u == 3 and t > 0)
+                if u > 0 and t == 0:
+                    nc.scalar.activation(logs[:, u - 1, 0:3, :], mags[u - 1][:], ACT.Ln, bias=LN_FLOOR)
+        nc.scalar.activation(logs[:, 3, 0:3, :], mags[3][:], ACT.Ln, bias=LN_FLOOR)
         for u in range(4):
             prey_magnitude(u, 3, gates[:, u, :], True)
         nc.scalar.activation(logs[:, :, 3, :], gates[:], ACT.Ln, bias=LN_FLOOR)
         pred_s = gather(tabs, list_pred, 0, S, U8, "pred_s", "s1")
-        pred_w = gather(tabw, list_pred, 0, S, U16, "pred_w", "w1")
-        round_w1(1)
+        pred_w = gather(tabw, list_pred, 0, S, U16, "pred_w", "early_b")
+        round_w1(1, w1_raw1)
         quantize_w1(1)
 
         w4w = keep.tile([P, 2, N], U16, name="w4w", tag="early_a", align_bytes=64)
         nc.sync.dma_start(w4w[:].bitcast(I32), w4_words.rearrange("a p c -> p a c").bitcast(I32))
-        w4s = keep.tile([P, 2, N], U8, name="w4s", tag="early_b", align_bytes=64)
+        w4s = keep.tile([P, 2, N], U8, name="w4s", tag="s0", align_bytes=64)
         nc.gpsimd.memset(w4s[:].bitcast(I32), 0)
         for q in range(4):
             nc.sync.dma_start(
@@ -176,23 +181,13 @@ def tile_list_trophic_link_energy_kernel(
             )
             return bank
 
-        def make_h(u, banks, c0, width):
-            a = UNITS[u][1]
-            cols = slice(c0, c0 + width)
-            resp = ring.tile([P, 4, width], F32, name="resp")
-            nc.scalar.activation(resp[:], logs[:, u, :, cols], ACT.Sigmoid, scale=2.0)
-            planes = ring.tile([P, 4, width], BF16, name="planes")
-            for t in range(4):
-                nc.scalar.activation(gates[:, t, cols], banks[t][:, cols], ACT.Sigmoid)
-                nc.vector.scalar_tensor_tensor(
-                    planes[:, t, :], resp[:, t, :], gains[:, a, t : t + 1], gates[:, t, cols], ALU.mult, ALU.mult
-                )
+        def weave(planes, width):
             woven = ring.tile([P, 4 * width], BF16, name="woven", align_bytes=64)
             nc.vector.tensor_copy(
                 woven[:].rearrange("p (c i t) -> p c t i", i=4, t=4),
                 planes[:].rearrange("p t (c i) -> p c t i", i=4),
             )
-            nc.vector.quantize_mx(hw[u][:, cols].bitcast(FP8X4), hs[u][:, cols], woven[:])
+            return woven
 
         def convert(dest, nt, u, cols, start, stop):
             a = UNITS[u][1]
@@ -215,22 +210,7 @@ def tile_list_trophic_link_energy_kernel(
             nc.sync.dma_start(dest, result[:].rearrange("p (n j) -> p n j", n=dest.shape[1]))
 
         out_rows = out.rearrange("(n p) j -> p n j", p=P)
-        for u in range(3):
-            make_h(u, [predator_product(u, t) for t in range(4)], 0, W)
-        for nt in range(4):
-            bank = psum.tile([P, W], F32, name="bank")
-            convert(bank[:], nt, 0, slice(0, W), True, False)
-            convert(bank[:], nt, 1, slice(0, W), False, True)
-            leave(bank, out_rows[:, nt : nt + 1, 0:W], nt % 2 == 1, f"result0_{nt}")
-
-        last_banks = [predator_product(3, t) for t in range(4)]
         sums = []
-        for c0, width in TAIL:
-            per_bank = W // width
-            for n0 in range(0, 4, per_bank):
-                bank = (psum_v if width == 256 else psum).tile([P, W], F32, name="bank")
-                pieces = [(i, j0) for i in range(per_bank) for j0 in range(0, width, P)]
-                sums.append((bank, c0, width, n0, per_bank, pieces))
 
         def convert_pieces(u, entry):
             bank, c0, width, n0, per_bank, pieces = entry
@@ -240,12 +220,48 @@ def tile_list_trophic_link_energy_kernel(
                     u == 2 and k == 0, u == 3 and k == len(pieces) - 1,
                 )
 
-        for entry in sums:
-            convert_pieces(2, entry)
-        for c0, width in TAIL:
-            make_h(3, last_banks, c0, width)
-            for entry in sums:
-                if entry[1] == c0:
-                    convert_pieces(3, entry)
+        def quantize_and_convert(u, c0, width, woven):
+            cols = slice(c0, c0 + width)
+            nc.vector.quantize_mx(hw[u][:, cols].bitcast(FP8X4), hs[u][:, cols], woven[:])
+            if u == 1:
+                for nt in range(4):
+                    bank = psum.tile([P, W], F32, name="bank")
+                    convert(bank[:], nt, 0, slice(0, W), True, False)
+                    convert(bank[:], nt, 1, slice(0, W), False, True)
+                    leave(bank, out_rows[:, nt : nt + 1, 0:W], nt % 2 == 1, f"result0_{nt}")
+            if u == 2:
+                for t0, tail_width in TAIL:
+                    per_bank = W // tail_width
+                    for n0 in range(0, 4, per_bank):
+                        bank = (psum_v if tail_width == 256 else psum).tile([P, W], F32, name="bank")
+                        pieces = [(i, j0) for i in range(per_bank) for j0 in range(0, tail_width, P)]
+                        sums.append((bank, t0, tail_width, n0, per_bank, pieces))
+                        convert_pieces(2, sums[-1])
+            if u == 3:
+                for entry in sums:
+                    if entry[1] == c0:
+                        convert_pieces(3, entry)
+
+        chunks = [(0, 0, 256), (0, 256, 256), (1, 0, W), (2, 0, W)] + [(3, c0, width) for c0, width in TAIL]
+        before = None
+        for u, c0, width in chunks:
+            a = UNITS[u][1]
+            cols = slice(c0, c0 + width)
+            if c0 == 0:
+                banks = [predator_product(u, t) for t in range(4)]
+            resp = ring.tile([P, 4, width], F32, name="resp")
+            nc.scalar.activation(resp[:], logs[:, u, :, cols], ACT.Sigmoid, scale=2.0)
+            planes = ring.tile([P, 4, width], BF16, name="planes")
+            for t in range(4):
+                nc.scalar.activation(gates[:, t, cols], banks[t][:, cols], ACT.Sigmoid)
+                nc.vector.scalar_tensor_tensor(
+                    planes[:, t, :], resp[:, t, :], gains[:, a, t : t + 1], gates[:, t, cols], ALU.mult, ALU.mult
+                )
+                if before is not None and t == 0:
+                    woven = weave(before[3], before[2])
+                if before is not None and t == 1:
+                    quantize_and_convert(before[0], before[1], before[2], woven)
+            before = (u, c0, width, planes)
+        quantize_and_convert(before[0], before[1], before[2], weave(before[3], before[2]))
         for k, (bank, c0, width, n0, per_bank, pieces) in enumerate(sums):
             leave(bank, out_rows[:, n0 : n0 + per_bank, W + c0 : W + c0 + width], k < len(sums) - 1, f"result1_{k}")

@@ -30,8 +30,8 @@ def tile_list_trophic_link_energy_kernel(
         keep = ctx.enter_context(tc.tile_pool(name="keep", bufs=1))
         ring = ctx.enter_context(tc.tile_pool(name="ring", bufs=2))
         ring3 = ctx.enter_context(tc.tile_pool(name="ring3", bufs=4))
-        psum = ctx.enter_context(tc.psum_pool(name="psum", bufs=6))
-        psum_v = ctx.enter_context(tc.psum_pool(name="psum_v", bufs=2))
+        psum = ctx.enter_context(tc.psum_pool(name="psum", bufs=5))
+        psum_v = ctx.enter_context(tc.psum_pool(name="psum_v", bufs=3))
 
         list_pred = keep.tile([P, S // 16], U16, name="list_pred")
         list_prey = keep.tile([P, S // 16], U16, name="list_prey")
@@ -96,9 +96,9 @@ def tile_list_trophic_link_energy_kernel(
         logs = keep.tile([P, 4, 4, W], F32, name="logs")
         gates = keep.tile([P, 4, W], F32, name="gates")
 
-        def prey_magnitude(u, t, dest, on_vector):
+        def prey_product(u, t, pool):
             jh, a = UNITS[u]
-            bank = (psum_v if on_vector else psum).tile([P, W], F32, name="bank")
+            bank = pool.tile([P, W], F32, name="bank")
             nc.tensor.matmul_mx(
                 bank[:],
                 lhsT=w8w[a][:, t * P : (t + 1) * P].bitcast(FP8X4),
@@ -108,12 +108,7 @@ def tile_list_trophic_link_energy_kernel(
                 start=True,
                 stop=True,
             )
-            if on_vector:
-                negated = ring.tile([P, W], F32, name="negated", align_bytes=64)
-                nc.vector.tensor_scalar(negated[:], bank[:], -1.0, None, ALU.mult)
-                nc.vector.tensor_tensor(dest, bank[:], negated[:], ALU.max)
-            else:
-                nc.scalar.activation(dest, bank[:], ACT.Abs)
+            return bank
 
         w1w, w1s, w1_grouped = [], [], []
 
@@ -138,16 +133,23 @@ def tile_list_trophic_link_energy_kernel(
         round_w1(0, load_w1(0))
         quantize_w1(0)
         w1_raw1 = load_w1(1)
-        mags = []
+        mags = [ring3.tile([P, 3, W], F32, name="mags") for u in range(4)]
         for u in range(4):
-            mags.append(ring3.tile([P, 3, W], F32, name="mags"))
-            for t in range(3):
-                prey_magnitude(u, t, mags[u][:, t, :], u == 3 and t > 0)
+            for t in range(3 if u < 3 else 1):
+                nc.scalar.activation(mags[u][:, t, :], prey_product(u, t, psum)[:], ACT.Abs)
                 if u > 0 and t == 0:
                     nc.scalar.activation(logs[:, u - 1, 0:3, :], mags[u - 1][:], ACT.Ln, bias=LN_FLOOR)
+        on_vector = [(3, t, mags[3][:, t, :]) for t in (1, 2)] + [(u, 3, gates[:, u, :]) for u in range(4)]
+        pending = None
+        for u, t, dest in on_vector:
+            bank = prey_product(u, t, psum_v)
+            negated = ring.tile([P, W], F32, name="negated", align_bytes=64)
+            nc.vector.tensor_scalar(negated[:], bank[:], -1.0, None, ALU.mult)
+            if pending is not None:
+                nc.vector.tensor_tensor(*pending, ALU.max)
+            pending = (dest, bank[:], negated[:])
+        nc.vector.tensor_tensor(*pending, ALU.max)
         nc.scalar.activation(logs[:, 3, 0:3, :], mags[3][:], ACT.Ln, bias=LN_FLOOR)
-        for u in range(4):
-            prey_magnitude(u, 3, gates[:, u, :], True)
         nc.scalar.activation(logs[:, :, 3, :], gates[:], ACT.Ln, bias=LN_FLOOR)
         pred_s = gather(tabs, list_pred, 0, S, U8, "pred_s", "s1")
         pred_w = gather(tabw, list_pred, 0, S, U16, "pred_w", "early_b")
@@ -225,7 +227,7 @@ def tile_list_trophic_link_energy_kernel(
             nc.vector.quantize_mx(hw[u][:, cols].bitcast(FP8X4), hs[u][:, cols], woven[:])
             if u == 1:
                 for nt in range(4):
-                    bank = psum.tile([P, W], F32, name="bank")
+                    bank = psum_v.tile([P, W], F32, name="bank")
                     convert(bank[:], nt, 0, slice(0, W), True, False)
                     convert(bank[:], nt, 1, slice(0, W), False, True)
                     leave(bank, out_rows[:, nt : nt + 1, 0:W], nt % 2 == 1, f"result0_{nt}")
@@ -233,7 +235,7 @@ def tile_list_trophic_link_energy_kernel(
                 for t0, tail_width in TAIL:
                     per_bank = W // tail_width
                     for n0 in range(0, 4, per_bank):
-                        bank = (psum_v if tail_width == 256 else psum).tile([P, W], F32, name="bank")
+                        bank = (psum_v if len(sums) < 3 else psum).tile([P, W], F32, name="bank")
                         pieces = [(i, j0) for i in range(per_bank) for j0 in range(0, tail_width, P)]
                         sums.append((bank, t0, tail_width, n0, per_bank, pieces))
                         convert_pieces(2, sums[-1])

from contextlib import ExitStack

import concourse.mybir as mybir

K, H, N, T, S = 512, 1024, 512, 4096, 1024
FLOPS = 2 * K * H * S * 2 + 2 * H * N * S

F32 = mybir.dt.float32
BF16 = mybir.dt.bfloat16
I32 = mybir.dt.int32
U16 = mybir.dt.uint16
U8 = mybir.dt.uint8
FP8X4 = mybir.dt.float8_e4m3fn_x4
FP4X4 = mybir.dt.float4_e2m1fn_x4
ACT = mybir.ActivationFunctionType
ALU = mybir.AluOpType

P = 128
W = 512
LN_FLOOR = 2.0 ** -60
UNITS = [(jh, a) for jh in range(2) for a in range(2)]
TAIL = [(0, 256), (256, 128), (384, 128)]


def tile_list_trophic_link_energy_kernel(
    tc, tab_words, tab_scales, offs, offs2, w1, w8_words, w8_scales, w4_words, w4_scales, gain, out
):
    nc = tc.nc
    with ExitStack() as ctx:
        keep = ctx.enter_context(tc.tile_pool(name="keep", bufs=1))
        ring = ctx.enter_context(tc.tile_pool(name="ring", bufs=2))
        ring3 = ctx.enter_context(tc.tile_pool(name="ring3", bufs=4))
        psum = ctx.enter_context(tc.psum_pool(name="psum", bufs=5))
        psum_v = ctx.enter_context(tc.psum_pool(name="psum_v", bufs=3))

        list_pred = keep.tile([P, S // 16], U16, name="list_pred")
        list_prey = keep.tile([P, S // 16], U16, name="list_prey")
        tabw = keep.tile([P, T], U16, name="tabw", align_bytes=64)
        tabs = keep.tile([P, T], U8, name="tabs", align_bytes=64)
        w8s_raw = keep.tile([P, H], U8, name="w8s_raw", tag="early_a", align_bytes=64)
        ones = keep.tile([P, 1], F32, name="ones")
        warm = keep.tile([P, 1], F32, name="warm")

        nc.gpsimd.memset(w8s_raw[:].bitcast(I32), 0)
        nc.vector.memset(tabs[:].bitcast(I32), 0)
        nc.vector.memset(ones[:], 1.0)

        w8_rows = w8_words[0].rearrange("p n t -> p (n t)").bitcast(I32)

        def load_w8(a):
            raw = keep.tile([P, W], I32, name=f"w8w_raw{a}", tag="early_b", align_bytes=64)
            nc.sync.dma_start(raw[:], w8_rows[:, a * W : (a + 1) * W])
            return raw

        def reorder_w8(a, raw):
            words = keep.tile([P, W], I32, name=f"w8w{a}", align_bytes=64)
            nc.vector.tensor_copy(words[:].rearrange("p (t m) -> p m t", t=4), raw[:].rearrange("p (m t) -> p m t", t=4))
            return words

        nc.sync.dma_start(list_prey[:], offs2)
        nc.sync.dma_start(list_pred[:], offs)
        w8w_raw0 = load_w8(0)
        nc.sync.dma_start(tabw[:].bitcast(I32), tab_words[0].bitcast(I32))
        for q in range(4):
            (nc.scalar if q < 2 else nc.gpsimd).dma_start(w8s_raw[32 * q : 32 * q + 4, :].bitcast(I32), w8_scales[0, 4 * q : 4 * q + 4, :].bitcast(I32))
        for q in range(4):
            nc.sync.dma_start(tabs[32 * q : 32 * q + 4, :].bitcast(I32), tab_scales[0, 4 * q : 4 * q + 4, :].bitcast(I32))
        nc.scalar.activation(warm[:], ones[:], ACT.Ln)
        gains = keep.tile([P, 2, 4], F32, name="gains", tag="ones")
        nc.gpsimd.dma_start(gains[:], gain.rearrange("(a p t) -> p a t", a=2, t=4))

        def gather(window, offsets, first, count, dtype, name, tag):
            picked = keep.tile([P, count], dtype, name=name, tag=tag, align_bytes=64)
            nc.vector.tensor_copy(picked[:], window[:].indirect(offsets[:, first // 16 : (first + count) // 16]))
            return picked

        prey_s, prey_w = {}, {}
        def reorder_w8_scales(a):
            scales = keep.tile([P, W], U8, name=f"w8s{a}", align_bytes=64)
            nc.vector.tensor_copy(
                scales[:].rearrange("p (t m) -> p m t", t=4), w8s_raw[:, a * W : (a + 1) * W].rearrange("p (m t) -> p m t", t=4)
            )
            return scales

        w8s = [reorder_w8_scales(0)]
        w8w = [reorder_w8(0, w8w_raw0)]
        prey_w[0] = gather(tabw, list_prey, 0, W, U16, "prey_w0", "w0")
        prey_s[0] = gather(tabs, list_prey, 0, W, U8, "prey_s0", "s0")
        w8s.append(reorder_w8_scales(1))
        w8w.append(reorder_w8(1, load_w8(1)))
        prey_s[1] = gather(tabs, list_prey, W, W, U8, "prey_s1", "s1")
        prey_w[1] = gather(tabw, list_prey, W, W, U16, "prey_w1", "early_b")

        w1_rows = w1.rearrange("(p j) c -> p j c", j=4)

        logs = keep.tile([P, 4, 4, W], F32, name="logs")
        gates = keep.tile([P, 4, W], F32, name="gates")

        def prey_product(u, t, pool):
            jh, a = UNITS[u]
            bank = pool.tile([P, W], F32, name="bank")
            nc.tensor.matmul_mx(
                bank[:],
                lhsT=w8w[a][:, t * P : (t + 1) * P].bitcast(FP8X4),
                lhsT_scale=w8s[a][:, t * P : (t + 1) * P],
                rhs=prey_w[jh][:].bitcast(FP4X4),
                rhs_scale=prey_s[jh][:],
                start=True,
                stop=True,
            )
            return bank

        w1w, w1s, w1_grouped = [], [], []

        def load_w1(a):
            raw = keep.tile([P, 4, W], F32, name=f"w1_raw{a}", tag="early_a", align_bytes=64)
            nc.sync.dma_start(raw[:], w1_rows[:, :, a * W : (a + 1) * W])
            return raw

        def round_w1(a, raw):
            grouped = ring.tile([P, 4 * W], BF16, name="w1_grouped", tag=("w1_grouped", "negated")[a], align_bytes=64)
            nc.vector.tensor_copy(
                grouped[:].rearrange("p (t m j) -> p m j t", t=4, j=4),
                raw[:].rearrange("p j (m t) -> p m j t", t=4),
            )
            w1_grouped.append(grouped)

        def quantize_w1(a):
            w1w.append(keep.tile([P, W], I32, name=f"w1w{a}", align_bytes=64))
            w1s.append(keep.tile([P, W], U8, name=f"w1s{a}", align_bytes=64))
            nc.vector.quantize_mx(w1w[a][:].bitcast(FP8X4), w1s[a][:], w1_grouped[a][:])

        round_w1(0, load_w1(0))
        quantize_w1(0)
        w1_raw1 = load_w1(1)
        mags = [ring3.tile([P, 3, W], F32, name="mags") for u in range(4)]
        for u in range(4):
            for t in range(3 if u < 3 else 1):
                nc.scalar.activation(mags[u][:, t, :], prey_product(u, t, psum)[:], ACT.Abs)
                if u > 0 and t == 0:
                    nc.scalar.activation(logs[:, u - 1, 0:3, :], mags[u - 1][:], ACT.Ln, bias=LN_FLOOR)
        on_vector = [(3, t, mags[3][:, t, :]) for t in (1, 2)] + [(u, 3, gates[:, u, :]) for u in range(4)]
        pending = None
        for u, t, dest in on_vector:
            bank = prey_product(u, t, psum_v)
            negated = ring.tile([P, W], F32, name="negated", align_bytes=64)
            nc.vector.tensor_scalar(negated[:], bank[:], -1.0, None, ALU.mult)
            if pending is not None:
                nc.vector.tensor_tensor(*pending, ALU.max)
            pending = (dest, bank[:], negated[:])
        nc.vector.tensor_tensor(*pending, ALU.max)
        nc.scalar.activation(logs[:, 3, 0:3, :], mags[3][:], ACT.Ln, bias=LN_FLOOR)
        nc.scalar.activation(logs[:, :, 3, :], gates[:], ACT.Ln, bias=LN_FLOOR)
        pred_s = gather(tabs, list_pred, 0, S, U8, "pred_s", "s1")
        pred_w = gather(tabw, list_pred, 0, S, U16, "pred_w", "early_b")
        round_w1(1, w1_raw1)
        quantize_w1(1)

        w4w = keep.tile([P, 2, N], U16, name="w4w", tag="early_a", align_bytes=64)
        nc.sync.dma_start(w4w[:].bitcast(I32), w4_words.rearrange("a p c -> p a c").bitcast(I32))
        w4s = keep.tile([P, 2, N], U8, name="w4s", tag="s0", align_bytes=64)
        nc.gpsimd.memset(w4s[:].bitcast(I32), 0)
        for q in range(4):
            nc.sync.dma_start(
                w4s[32 * q : 32 * q + 4, :, :].bitcast(I32),
                w4_scales[:, 4 * q : 4 * q + 4, :].rearrange("a r c -> r a c").bitcast(I32),
            )

        hw = [keep.tile([P, W], I32, name=f"hw{u}", align_bytes=64) for u in range(4)]
        hs = [keep.tile([P, W], U8, name=f"hs{u}", align_bytes=64) for u in range(4)]

        def predator_product(u, t):
            jh, a = UNITS[u]
            bank = psum.tile([P, W], F32, name="bank")
            nc.tensor.matmul_mx(
                bank[:],
                lhsT=w1w[a][:, t * P : (t + 1) * P].bitcast(FP8X4),
                lhsT_scale=w1s[a][:, t * P : (t + 1) * P],
                rhs=pred_w[:, jh * W : (jh + 1) * W].bitcast(FP4X4),
                rhs_scale=pred_s[:, jh * W : (jh + 1) * W],
                start=True,
                stop=True,
            )
            return bank

        def weave(planes, width):
            woven = ring.tile([P, 4 * width], BF16, name="woven", align_bytes=64)
            nc.vector.tensor_copy(
                woven[:].rearrange("p (c i t) -> p c t i", i=4, t=4),
                planes[:].rearrange("p t (c i) -> p c t i", i=4),
            )
            return woven

        def convert(dest, nt, u, cols, start, stop):
            a = UNITS[u][1]
            nc.tensor.matmul_mx(
                dest,
                lhsT=w4w[:, a, nt * P : (nt + 1) * P].bitcast(FP4X4),
                lhsT_scale=w4s[:, a, nt * P : (nt + 1) * P],
                rhs=hw[u][:, cols].bitcast(FP8X4),
                rhs_scale=hs[u][:, cols],
                start=start,
                stop=stop,
            )

        def leave(bank, dest, on_scalar, name):
            result = keep.tile([P, W], F32, name=name)
            if on_scalar:
                nc.scalar.copy(result[:], bank[:])
            else:
                nc.vector.tensor_copy(result[:], bank[:])
            nc.sync.dma_start(dest, result[:].rearrange("p (n j) -> p n j", n=dest.shape[1]))

        out_rows = out.rearrange("(n p) j -> p n j", p=P)
        sums = []

        def convert_pieces(u, entry):
            bank, c0, width, n0, per_bank, pieces = entry
            for k, (i, j0) in enumerate(pieces):
                convert(
                    bank[:, i * width + j0 : i * width + j0 + P], n0 + i, u, slice(c0 + j0, c0 + j0 + P),
                    u == 2 and k == 0, u == 3 and k == len(pieces) - 1,
                )

        def quantize_and_convert(u, c0, width, woven):
            cols = slice(c0, c0 + width)
            nc.vector.quantize_mx(hw[u][:, cols].bitcast(FP8X4), hs[u][:, cols], woven[:])
            if u == 1:
                for nt in range(4):
                    bank = psum_v.tile([P, W], F32, name="bank")
                    convert(bank[:], nt, 0, slice(0, W), True, False)
                    convert(bank[:], nt, 1, slice(0, W), False, True)
                    leave(bank, out_rows[:, nt : nt + 1, 0:W], nt % 2 == 1, f"result0_{nt}")
            if u == 2:
                for t0, tail_width in TAIL:
                    per_bank = W // tail_width
                    for n0 in range(0, 4, per_bank):
                        bank = (psum_v if len(sums) < 3 else psum).tile([P, W], F32, name="bank")
                        pieces = [(i, j0) for i in range(per_bank) for j0 in range(0, tail_width, P)]
                        sums.append((bank, t0, tail_width, n0, per_bank, pieces))
                        convert_pieces(2, sums[-1])
            if u == 3:
                for entry in sums:
                    if entry[1] == c0:
                        convert_pieces(3, entry)

        chunks = [(0, 0, 256), (0, 256, 256), (1, 0, W), (2, 0, W)] + [(3, c0, width) for c0, width in TAIL]
        before = None
        for u, c0, width in chunks:
            a = UNITS[u][1]
            cols = slice(c0, c0 + width)
            if c0 == 0:
                banks = [predator_product(u, t) for t in range(4)]
            resp = ring.tile([P, 4, width], F32, name="resp")
            nc.scalar.activation(resp[:], logs[:, u, :, cols], ACT.Sigmoid, scale=2.0)
            planes = ring.tile([P, 4, width], BF16, name="planes")
            for t in range(4):
                nc.scalar.activation(gates[:, t, cols], banks[t][:, cols], ACT.Sigmoid)
                nc.vector.scalar_tensor_tensor(
                    planes[:, t, :], resp[:, t, :], gains[:, a, t : t + 1], gates[:, t, cols], ALU.mult, ALU.mult
                )
                if before is not None and t == 0:
                    woven = weave(before[3], before[2])
                if before is not None and t == 1:
                    quantize_and_convert(before[0], before[1], before[2], woven)
            before = (u, c0, width, planes)
        quantize_and_convert(before[0], before[1], before[2], weave(before[3], before[2]))
        for k, (bank, c0, width, n0, per_bank, pieces) in enumerate(sums):
            leave(bank, out_rows[:, n0 : n0 + per_bank, W + c0 : W + c0 + width], k < len(sums) - 1, f"result1_{k}")
